import numpy as np
import ml_dtypes


def mxq(x, axis, fmt="e4m3"):
    dtype, down = {"e4m3": (ml_dtypes.float8_e4m3fn, 7), "e5m2": (ml_dtypes.float8_e5m2, 14)}[fmt]
    v = np.moveaxis(np.asarray(x, np.float32).astype(ml_dtypes.bfloat16).astype(np.float64), axis, -1)
    blocks = v.reshape(v.shape[:-1] + (-1, 32))
    amax = np.abs(blocks).max(-1, keepdims=True)
    byte = np.maximum(np.where(amax > 0, np.frexp(amax)[1] - 1 + 127, 0) - down, 1)
    scale = np.exp2(byte - 127.0)
    codes = (blocks / scale).astype(np.float32).astype(dtype).astype(np.float64)
    return np.moveaxis((codes * scale).reshape(v.shape), -1, axis)


WIDE = False


def mx_kscale(k):
    if not WIDE:
        return np.ones(k)
    levels = np.array([10, -10, 5, -5, 0])
    if k % 512:
        return np.exp2(np.random.permutation(np.resize(levels, k // 32))).repeat(32)
    a = np.empty((k // 512, 16))
    for p in range(k // 512):
        a[p, :8] = np.random.permutation(np.resize(levels, 8))
        for g in range(8):
            far = levels[np.abs(levels - a[p, g]) >= 10]
            a[p, g + 8] = far[np.random.randint(len(far))]
    return np.exp2(a.ravel()).repeat(32)


def f64(x):
    return np.asarray(x).astype(np.float64)


def striped(idx):
    return np.tile(idx.reshape(-1, 16).T, (8, 1)).astype(np.uint16)


def unstriped(offs):
    return offs[:16].T.reshape(-1).astype(np.int64)


def striped8(idx):
    return np.concatenate([x.reshape(-1, 16).T for x in idx]).astype(np.uint16)


def runs(offs, k):
    lists = np.stack([offs[16 * r : 16 * r + 16].T.reshape(-1) for r in range(8)]).astype(np.int64)
    return lists[np.arange(k) % 512 // 64]


def pack_weight(w):
    k, n = w.shape
    w = f64(np.asarray(w, np.float32).astype(ml_dtypes.bfloat16)).reshape(k // 32, 32, n)
    amax = np.abs(w).max(1)
    byte = np.clip(np.where(amax > 0, np.frexp(amax)[1] - 1 + 127 - 7, 1), 1, 254)
    scaled = (w * np.exp2(127.0 - byte)[:, None, :]).reshape(k, n).astype(np.float32)
    words = np.ascontiguousarray(scaled.reshape(k // 512, 128, 4, n).transpose(0, 1, 3, 2)).astype(ml_dtypes.float8_e4m3fn).view(np.uint8)
    return words, np.ascontiguousarray(byte.astype(np.uint8).reshape(k // 512, 16, n))


def unpack_weight(words, scales):
    g, p, n, _ = words.shape
    vals = np.ascontiguousarray(words).view(ml_dtypes.float8_e4m3fn).astype(np.float64) * np.repeat(np.exp2(scales.astype(np.float64) - 127.0), 8, axis=1)[..., None]
    return vals.transpose(0, 1, 3, 2).reshape(g * 512, n)


def sigmoid(v):
    return 1.0 / (1.0 + np.exp(-np.maximum(v, -700.0)))


K, T, S, N, H, W, U = 512, 2048, 512, 512, 512, 256, 1024


def setup_inputs():
    n = np.random.standard_normal
    s = mx_kscale(K)[:, None]
    u = mx_kscale(H)
    packed_xT = pack_weight(n((K, T)) * s)
    return {
        "x_words": packed_xT[0],
        "x_scales": packed_xT[1],
        "w1": (n((K, H)) / np.sqrt(K) / s).astype(np.float32),
        "w2": (n((K, H)) / np.sqrt(K) / s).astype(np.float32),
        "w3": (n((K, H)) / np.sqrt(K) / s).astype(np.float32),
        "gn": (np.random.uniform(0.5, 1.5, (H, 1)) * u[:, None]).astype(np.float32),
        "w4": (n((H, N)) / np.sqrt(H) / u[:, None]).astype(np.float32),
        "mem": n((N, U)).astype(np.float32),
        "offs": striped(np.random.permutation(T)[:S]),
        "two": striped(np.random.permutation(T)[:S]),
        "three": striped(np.random.permutation(T)[:S]),
        "n1": striped8(np.stack([np.random.permutation(S) for _ in range(8)])),
        "n2": striped8(np.stack([np.random.permutation(S) for _ in range(8)])),
        "n3": striped8(np.stack([np.random.permutation(S)[:W] for _ in range(8)])),
        "n4": striped8(np.stack([np.random.permutation(S)[:W] for _ in range(8)])),
        "n5": striped8(np.stack([np.random.permutation(U)[:S] for _ in range(8)])),
    }


def reference(x_words, x_scales, w1, w2, w3, gn, w4, mem, offs, two, three, n1, n2, n3, n4, n5):
    x_three = unpack_weight(x_words, x_scales)[:, unstriped(three)]
    b = mxq(f64(w3), 0, "e4m3").T @ x_three
    xq = unpack_weight(x_words, x_scales)[:, unstriped(offs)]
    y = mxq(f64(w1), 0, "e4m3").T @ xq
    x_two = unpack_weight(x_words, x_scales)[:, unstriped(two)]
    d = mxq(f64(w2), 0, "e4m3").T @ x_two
    m1 = y + (sigmoid(d[np.arange(H)[:, None], runs(n2, H)] - d)) * (y[np.arange(H)[:, None], runs(n1, H)] - y)
    ra = b[np.arange(H)[:, None], runs(n4, H)] - (0.5 * (m1[np.arange(H)[:, None], runs(n3, H)]))
    ds = m1.copy()
    ds[np.arange(H)[:, None], runs(n3, H)] = ra
    z = f64(gn) * ds
    h = mxq(f64(w4), 0, "e4m3").T @ mxq(z, 0, "e4m3")
    nw = np.maximum(h, 0.5 * (f64(mem)[np.arange(N)[:, None], runs(n5, N)]))
    out = f64(mem).copy()
    out[np.arange(N)[:, None], runs(n5, N)] = nw
    return out

@@ -1,0 +1,181 @@
+from contextlib import ExitStack
+
+import concourse.mybir as mybir
+
+K, T, S, N, H, W, U = 512, 2048, 512, 512, 512, 256, 1024
+FLOPS = 2 * 3 * K * H * S + 2 * H * N * S
+
+F32 = mybir.dt.float32
+BF16 = mybir.dt.bfloat16
+I32 = mybir.dt.int32
+U32 = mybir.dt.uint32
+U16 = mybir.dt.uint16
+U8 = mybir.dt.uint8
+FP8X4 = mybir.dt.float8_e4m3fn_x4
+ALU = mybir.AluOpType
+ACT = mybir.ActivationFunctionType
+
+P = 128
+PACK = 4
+HALF = S // 2
+
+
+def tile_picked_triopullbputbpagex_none_p_kernel(tc, x_words, x_scales, w1, w2, w3, gn, w4, mem, offs, two, three, n1, n2, n3, n4, n5, out):
+    nc = tc.nc
+    with ExitStack() as ctx:
+        lists = ctx.enter_context(tc.tile_pool(name="lists", bufs=1))
+        keep = ctx.enter_context(tc.tile_pool(name="keep", bufs=1))
+        psum = ctx.enter_context(tc.psum_pool(name="psum", bufs=8))
+
+        def load_list(name, src):
+            tile = lists.tile(list(src.shape), U16, name=name)
+            nc.sync.dma_start(tile[:], src)
+            return tile
+
+        def load_weight(name, src, queue):
+            raw = keep.tile([P, PACK, H], F32, name=name + "_raw")
+            queue.dma_start(out=raw[:], in_=src.rearrange("(p j) c -> p j c", j=PACK))
+            return raw
+
+        xs = keep.tile([P, T], U8, name="xs")
+        xw = keep.tile([P, T], I32, name="xw")
+        nc.vector.memset(xs[:].bitcast(I32), 0)
+
+        w2_raw = load_weight("w2", w2, nc.scalar)
+        l_two = load_list("l_two", two)
+        for q in range(4):
+            nc.sync.dma_start(out=xs[32 * q : 32 * q + 4, :].bitcast(I32), in_=x_scales[0, 4 * q : 4 * q + 4, :].bitcast(I32))
+        l_offs = load_list("l_offs", offs)
+        nc.sync.dma_start(out=xw[:], in_=x_words[0].rearrange("p n t -> p (n t)").bitcast(I32))
+        l_three = load_list("l_three", three)
+        w1_raw = load_weight("w1", w1, nc.sync)
+        l_n2 = load_list("l_n2", n2)
+        l_n1 = load_list("l_n1", n1)
+        gain = keep.tile([P, PACK], F32, name="gain")
+        nc.sync.dma_start(out=gain[:], in_=gn.rearrange("(p t) o -> p (t o)", t=PACK))
+        w3_raw = load_weight("w3", w3, nc.sync)
+        l_n4 = load_list("l_n4", n4)
+        l_n3 = load_list("l_n3", n3)
+        l_n5 = load_list("l_n5", n5)
+        w4_raw = load_weight("w4", w4, nc.sync)
+        mem_rows = mem.rearrange("(p t) u -> t p u", t=PACK)
+        out_rows = out.rearrange("(p t) u -> t p u", t=PACK)
+        pages = []
+        for t in range(PACK):
+            page = keep.tile([P, U], F32, name=f"page{t}")
+            nc.sync.dma_start(out=page[:], in_=mem_rows[t])
+            pages.append(page)
+
+        def pick_scales(name, offsets):
+            picked = keep.tile([P, S], U8, name=name + "_scales", align_bytes=64)
+            nc.vector.tensor_copy(picked[:], xs[:].indirect(offsets[:]))
+            return picked
+
+        def pick_words(name, offsets):
+            picked = keep.tile([P, S], U32, name=name + "_words", align_bytes=64)
+            nc.vector.tensor_copy(picked[:], xw[:].bitcast(U32).indirect(offsets[:]))
+            return picked
+
+        def round_weight(name, raw):
+            grouped = keep.tile([P, PACK * H], BF16, name=name + "_grouped", align_bytes=64)
+            nc.scalar.copy(
+                out=grouped[:].rearrange("p (t m j) -> p m j t", t=PACK, j=PACK),
+                in_=raw[:].rearrange("p j (m t) -> p m j t", t=PACK),
+            )
+            return grouped
+
+        def quantize(name, grouped):
+            codes = keep.tile([P, H], U32, name=name + "_codes", align_bytes=64)
+            scales = keep.tile([P, H], U8, name=name + "_qs", align_bytes=64)
+            nc.vector.quantize_mx(out=codes[:].bitcast(FP8X4), scales=scales[:], in_=grouped[:])
+            return codes, scales
+
+        def product(weight, moving, t):
+            acc = psum.tile([P, S], F32, name="acc")
+            cols = slice(P * t, P * (t + 1))
+            nc.tensor.matmul_mx(
+                out=acc[:],
+                lhsT=weight[0][:, cols].bitcast(FP8X4),
+                lhsT_scale=weight[1][:, cols],
+                rhs=moving[0][:].bitcast(FP8X4),
+                rhs_scale=moving[1][:],
+                start=True,
+                stop=True,
+            )
+            return acc
+
+        s_two = pick_scales("two", l_two)
+        s_offs = pick_scales("offs", l_offs)
+        s_three = pick_scales("three", l_three)
+        x_two = (pick_words("two", l_two), s_two)
+        q2 = quantize("w2", round_weight("w2", w2_raw))
+        x_offs = (pick_words("offs", l_offs), s_offs)
+        x_three = (pick_words("three", l_three), s_three)
+
+        def minus_own(name, window, own, offsets):
+            diff = keep.tile([P, S], F32, name=name)
+            for a in range(2):
+                cols = slice(HALF * a, HALF * (a + 1))
+                nc.vector.tensor_tensor(diff[:, cols], window[:].indirect(offsets[:, 16 * a : 16 * (a + 1)]), own[:, cols], ALU.subtract)
+            return diff
+
+        gates = []
+        for t in range(PACK):
+            acc = product(q2, x_two, t)
+            d_win = keep.tile([P, S], F32, name=f"d_win{t}")
+            d_own = keep.tile([P, S], F32, name=f"d_own{t}")
+            nc.scalar.copy(out=d_win[:], in_=acc[:])
+            nc.scalar.copy(out=d_own[:], in_=acc[:])
+            dd = minus_own(f"dd{t}", d_win, d_own, l_n2)
+            gates.append(dd)
+
+        q1 = quantize("w1", round_weight("w1", w1_raw))
+        ys = []
+        for t in range(PACK):
+            acc = product(q1, x_offs, t)
+            y_win = keep.tile([P, S], F32, name=f"y_win{t}")
+            y_own = keep.tile([P, S], F32, name=f"y_own{t}")
+            nc.scalar.activation(y_win[:], acc[:], ACT.Copy, scale=gain[:, t : t + 1])
+            nc.scalar.activation(y_own[:], acc[:], ACT.Copy, scale=gain[:, t : t + 1])
+            dy = minus_own(f"dy{t}", y_win, y_own, l_n1)
+            nc.scalar.activation(gates[t][:], gates[t][:], ACT.Sigmoid)
+            ys.append((y_own, dy))
+
+        q3 = quantize("w3", round_weight("w3", w3_raw))
+        zg = keep.tile([P, S, PACK], BF16, name="zg", tag="zg", align_bytes=64)
+        for t in range(PACK):
+            y_own, dy = ys[t]
+            nc.vector.tensor_tensor(dy[:], dy[:], gates[t][:], ALU.mult)
+            acc = product(q3, x_three, t)
+            b_win = keep.tile([P, S], F32, name=f"b_win{t}")
+            nc.scalar.activation(b_win[:], acc[:], ACT.Copy, scale=gain[:, t : t + 1])
+            b_picked = keep.tile([P, W], F32, name=f"b_picked{t}", tag=f"b_picked{t}")
+            nc.vector.tensor_copy(b_picked[:], b_win[:].indirect(l_n4[:]))
+            m1 = keep.tile([P, S], F32, name=f"m1_{t}")
+            nc.vector.tensor_tensor(m1[:], dy[:], y_own[:], ALU.add)
+            m_picked = keep.tile([P, W], F32, name=f"m_picked{t}", tag=f"m_picked{t}")
+            nc.vector.tensor_scalar(m_picked[:], m1[:].indirect(l_n3[:]), -0.5, 0.0, ALU.mult, ALU.add)
+            nc.vector.tensor_tensor(m1[:].indirect(l_n3[:]), b_picked[:], m_picked[:], ALU.add)
+            nc.scalar.copy(out=zg[:, :, t], in_=m1[:])
+
+        q4 = quantize("w4", round_weight("w4", w4_raw))
+        old0 = keep.tile([P, S], F32, name="old0", tag="b_picked3")
+        old1 = keep.tile([P, S], F32, name="old1", tag="m_picked3")
+        nc.vector.tensor_copy(old0[:], pages[0][:].indirect(l_n5[:]))
+        nc.vector.tensor_copy(old1[:], pages[1][:].indirect(l_n5[:]))
+        z_codes = keep.tile([P, S], U32, name="z_codes", align_bytes=64)
+        z_scales = keep.tile([P, S], U8, name="z_scales", align_bytes=64)
+        nc.vector.quantize_mx(out=z_codes[:].bitcast(FP8X4), scales=z_scales[:], in_=zg[:].rearrange("p s t -> p (s t)"))
+        old23 = keep.tile([P, 2, S], F32, name="old23", tag="zg", align_bytes=64)
+        nc.vector.tensor_copy(old23[:, 0, :], pages[2][:].indirect(l_n5[:]))
+        nc.vector.tensor_copy(old23[:, 1, :], pages[3][:].indirect(l_n5[:]))
+        olds = [old0[:], old1[:], old23[:, 0, :], old23[:, 1, :]]
+        news = []
+        for t in range(PACK):
+            acc = product(q4, (z_codes, z_scales), t)
+            new = keep.tile([P, S], F32, name=f"new{t}")
+            nc.vector.scalar_tensor_tensor(new[:], olds[t], 0.5, acc[:], ALU.mult, ALU.max)
+            news.append(new)
+        for t in range(PACK):
+            nc.vector.tensor_copy(pages[t][:].indirect(l_n5[:]), news[t][:])
+            nc.sync.dma_start(out=out_rows[t], in_=pages[t][:])

@@ -25,7 +25,7 @@ def tile_picked_triopullbputbpagex_none_p_kernel(tc, x_words, x_scales, w1, w2, 
     with ExitStack() as ctx:
         lists = ctx.enter_context(tc.tile_pool(name="lists", bufs=1))
         keep = ctx.enter_context(tc.tile_pool(name="keep", bufs=1))
-        psum = ctx.enter_context(tc.psum_pool(name="psum", bufs=8))
+        psum = ctx.enter_context(tc.psum_pool(name="psum", bufs=1))
 
         def load_list(name, src):
             tile = lists.tile(list(src.shape), U16, name=name)
@@ -33,20 +33,23 @@ def tile_picked_triopullbputbpagex_none_p_kernel(tc, x_words, x_scales, w1, w2, 
             return tile
 
         def load_weight(name, src, queue):
-            raw = keep.tile([P, PACK, H], F32, name=name + "_raw")
+            raw = keep.tile([P, PACK, H], F32, name=name + "_raw", tag=name + "_raw", align_bytes=64)
             queue.dma_start(out=raw[:], in_=src.rearrange("(p j) c -> p j c", j=PACK))
             return raw
 
         xs = keep.tile([P, T], U8, name="xs")
         xw = keep.tile([P, T], I32, name="xw")
-        nc.vector.memset(xs[:].bitcast(I32), 0)
+        nc.gpsimd.memset(xs[:].bitcast(I32), 0)
 
-        w2_raw = load_weight("w2", w2, nc.scalar)
         l_two = load_list("l_two", two)
-        for q in range(4):
-            nc.sync.dma_start(out=xs[32 * q : 32 * q + 4, :].bitcast(I32), in_=x_scales[0, 4 * q : 4 * q + 4, :].bitcast(I32))
-        l_offs = load_list("l_offs", offs)
         nc.sync.dma_start(out=xw[:], in_=x_words[0].rearrange("p n t -> p (n t)").bitcast(I32))
+        for q in range(4):
+            nc.scalar.dma_start(out=xs[32 * q : 32 * q + 4, :].bitcast(I32), in_=x_scales[0, 4 * q : 4 * q + 4, :].bitcast(I32))
+        warm = keep.tile([P, 2], F32, name="warm")
+        nc.gpsimd.memset(warm[:, 0:1], 0.0)
+        nc.scalar.activation(warm[:, 1:2], warm[:, 0:1], ACT.Sigmoid)
+        l_offs = load_list("l_offs", offs)
+        w2_raw = load_weight("w2", w2, nc.sync)
         l_three = load_list("l_three", three)
         w1_raw = load_weight("w1", w1, nc.sync)
         l_n2 = load_list("l_n2", n2)
@@ -71,13 +74,13 @@ def tile_picked_triopullbputbpagex_none_p_kernel(tc, x_words, x_scales, w1, w2, 
             nc.vector.tensor_copy(picked[:], xs[:].indirect(offsets[:]))
             return picked
 
-        def pick_words(name, offsets):
-            picked = keep.tile([P, S], U32, name=name + "_words", align_bytes=64)
+        def pick_words(name, offsets, tag):
+            picked = keep.tile([P, S], U32, name=name + "_words", tag=tag, align_bytes=64)
             nc.vector.tensor_copy(picked[:], xw[:].bitcast(U32).indirect(offsets[:]))
             return picked
 
-        def round_weight(name, raw):
-            grouped = keep.tile([P, PACK * H], BF16, name=name + "_grouped", align_bytes=64)
+        def round_weight(name, raw, tag):
+            grouped = keep.tile([P, PACK * H], BF16, name=name + "_grouped", tag=tag, align_bytes=64)
             nc.scalar.copy(
                 out=grouped[:].rearrange("p (t m j) -> p m j t", t=PACK, j=PACK),
                 in_=raw[:].rearrange("p j (m t) -> p m j t", t=PACK),
@@ -90,8 +93,8 @@ def tile_picked_triopullbputbpagex_none_p_kernel(tc, x_words, x_scales, w1, w2, 
             nc.vector.quantize_mx(out=codes[:].bitcast(FP8X4), scales=scales[:], in_=grouped[:])
             return codes, scales
 
-        def product(weight, moving, t):
-            acc = psum.tile([P, S], F32, name="acc")
+        def product(weight, moving, t, tag, depth):
+            acc = psum.tile([P, S], F32, name=tag, bufs=depth)
             cols = slice(P * t, P * (t + 1))
             nc.tensor.matmul_mx(
                 out=acc[:],
@@ -107,72 +110,81 @@ def tile_picked_triopullbputbpagex_none_p_kernel(tc, x_words, x_scales, w1, w2, 
         s_two = pick_scales("two", l_two)
         s_offs = pick_scales("offs", l_offs)
         s_three = pick_scales("three", l_three)
-        x_two = (pick_words("two", l_two), s_two)
-        q2 = quantize("w2", round_weight("w2", w2_raw))
-        x_offs = (pick_words("offs", l_offs), s_offs)
-        x_three = (pick_words("three", l_three), s_three)
+        x_two = (pick_words("two", l_two, "two_words"), s_two)
+        q2 = quantize("w2", round_weight("w2", w2_raw, "w2_grouped"))
+        x_offs = (pick_words("offs", l_offs, "offs_words"), s_offs)
+        x_three = (pick_words("three", l_three, "w2_grouped"), s_three)
 
-        def minus_own(name, window, own, offsets):
-            diff = keep.tile([P, S], F32, name=name)
+        def fetch(name, window, offsets, tag):
+            picked = keep.tile([P, S], F32, name=name, tag=tag, align_bytes=64)
             for a in range(2):
-                cols = slice(HALF * a, HALF * (a + 1))
-                nc.vector.tensor_tensor(diff[:, cols], window[:].indirect(offsets[:, 16 * a : 16 * (a + 1)]), own[:, cols], ALU.subtract)
-            return diff
+                nc.vector.tensor_copy(picked[:, HALF * a : HALF * (a + 1)], window[:].indirect(offsets[:, 16 * a : 16 * (a + 1)]))
+            return picked
 
+        q1 = quantize("w1", round_weight("w1", w1_raw, "w1_grouped"))
         gates = []
         for t in range(PACK):
-            acc = product(q2, x_two, t)
-            d_win = keep.tile([P, S], F32, name=f"d_win{t}")
-            d_own = keep.tile([P, S], F32, name=f"d_own{t}")
+            acc = product(q2, x_two, t, "d_acc", 2)
+            d_win = keep.tile([P, S], F32, name=f"d_win{t}", tag=("w1_raw", "w1_grouped", "d_win2", "d_win3")[t], align_bytes=64)
             nc.scalar.copy(out=d_win[:], in_=acc[:])
-            nc.scalar.copy(out=d_own[:], in_=acc[:])
-            dd = minus_own(f"dd{t}", d_win, d_own, l_n2)
+            dd = fetch(f"dd{t}", d_win, l_n2, f"dd{t}")
+            nc.gpsimd.tensor_tensor(dd[:], dd[:], d_win[:], ALU.subtract)
             gates.append(dd)
 
-        q1 = quantize("w1", round_weight("w1", w1_raw))
-        ys = []
-        for t in range(PACK):
-            acc = product(q1, x_offs, t)
-            y_win = keep.tile([P, S], F32, name=f"y_win{t}")
-            y_own = keep.tile([P, S], F32, name=f"y_own{t}")
-            nc.scalar.activation(y_win[:], acc[:], ACT.Copy, scale=gain[:, t : t + 1])
-            nc.scalar.activation(y_own[:], acc[:], ACT.Copy, scale=gain[:, t : t + 1])
-            dy = minus_own(f"dy{t}", y_win, y_own, l_n1)
-            nc.scalar.activation(gates[t][:], gates[t][:], ACT.Sigmoid)
-            ys.append((y_own, dy))
-
-        q3 = quantize("w3", round_weight("w3", w3_raw))
         zg = keep.tile([P, S, PACK], BF16, name="zg", tag="zg", align_bytes=64)
+        dys = []
+        y_wins = []
         for t in range(PACK):
-            y_own, dy = ys[t]
-            nc.vector.tensor_tensor(dy[:], dy[:], gates[t][:], ALU.mult)
-            acc = product(q3, x_three, t)
-            b_win = keep.tile([P, S], F32, name=f"b_win{t}")
+            acc = product(q1, x_offs, t, "acc", 6)
+            y_win = keep.tile([P, S], F32, name=f"y_win{t}")
+            nc.scalar.activation(y_win[:], acc[:], ACT.Copy, scale=gain[:, t : t + 1])
+            y_wins.append(y_win)
+        for t in range(PACK - 1):
+            dys.append((y_wins[t], fetch(f"dy{t}", y_wins[t], l_n1, f"dy{t}")))
+        q3 = quantize("w3", round_weight("w3", w3_raw, "w1_grouped"))
+        dys.append((y_wins[3], fetch("dy3", y_wins[3], l_n1, "w1_grouped")))
+        for t in range(PACK):
+            nc.scalar.activation(gates[t][:], gates[t][:], ACT.Sigmoid)
+        bs = []
+        for t in range(PACK):
+            acc = product(q3, x_three, t, "acc", 6)
+            b_win = keep.tile([P, S], F32, name=f"b_win{t}", tag=f"b_win{t}", align_bytes=64)
             nc.scalar.activation(b_win[:], acc[:], ACT.Copy, scale=gain[:, t : t + 1])
             b_picked = keep.tile([P, W], F32, name=f"b_picked{t}", tag=f"b_picked{t}")
             nc.vector.tensor_copy(b_picked[:], b_win[:].indirect(l_n4[:]))
+            bs.append(b_picked)
+        for t in range(PACK):
+            y_win, dy = dys[t]
+            last = t >= PACK - 2
+            nc.gpsimd.tensor_tensor(dy[:], dy[:], y_win[:], ALU.subtract)
+            nc.gpsimd.tensor_tensor(dy[:], dy[:], gates[t][:], ALU.mult)
             m1 = keep.tile([P, S], F32, name=f"m1_{t}")
-            nc.vector.tensor_tensor(m1[:], dy[:], y_own[:], ALU.add)
+            (nc.vector if last else nc.gpsimd).tensor_tensor(m1[:], dy[:], y_win[:], ALU.add)
             m_picked = keep.tile([P, W], F32, name=f"m_picked{t}", tag=f"m_picked{t}")
             nc.vector.tensor_scalar(m_picked[:], m1[:].indirect(l_n3[:]), -0.5, 0.0, ALU.mult, ALU.add)
-            nc.vector.tensor_tensor(m1[:].indirect(l_n3[:]), b_picked[:], m_picked[:], ALU.add)
+            if last:
+                nc.vector.tensor_tensor(m1[:].indirect(l_n3[:]), m_picked[:], bs[t][:], ALU.add)
+            else:
+                nc.gpsimd.tensor_tensor(m_picked[:], m_picked[:], bs[t][:], ALU.add)
+                nc.vector.tensor_copy(m1[:].indirect(l_n3[:]), m_picked[:])
             nc.scalar.copy(out=zg[:, :, t], in_=m1[:])
 
-        q4 = quantize("w4", round_weight("w4", w4_raw))
-        old0 = keep.tile([P, S], F32, name="old0", tag="b_picked3")
-        old1 = keep.tile([P, S], F32, name="old1", tag="m_picked3")
+        q4 = quantize("w4", round_weight("w4", w4_raw, "d_win3"))
+        old0 = keep.tile([P, S], F32, name="old0", tag="dy1", align_bytes=64)
+        old1 = keep.tile([P, S], F32, name="old1", tag="b_picked3")
+        old2 = keep.tile([P, S], F32, name="old2", tag="m_picked3")
         nc.vector.tensor_copy(old0[:], pages[0][:].indirect(l_n5[:]))
         nc.vector.tensor_copy(old1[:], pages[1][:].indirect(l_n5[:]))
+        nc.vector.tensor_copy(old2[:], pages[2][:].indirect(l_n5[:]))
         z_codes = keep.tile([P, S], U32, name="z_codes", align_bytes=64)
         z_scales = keep.tile([P, S], U8, name="z_scales", align_bytes=64)
         nc.vector.quantize_mx(out=z_codes[:].bitcast(FP8X4), scales=z_scales[:], in_=zg[:].rearrange("p s t -> p (s t)"))
-        old23 = keep.tile([P, 2, S], F32, name="old23", tag="zg", align_bytes=64)
-        nc.vector.tensor_copy(old23[:, 0, :], pages[2][:].indirect(l_n5[:]))
-        nc.vector.tensor_copy(old23[:, 1, :], pages[3][:].indirect(l_n5[:]))
-        olds = [old0[:], old1[:], old23[:, 0, :], old23[:, 1, :]]
+        old3 = keep.tile([P, S], F32, name="old3", tag="zg", align_bytes=64)
+        nc.vector.tensor_copy(old3[:], pages[3][:].indirect(l_n5[:]))
+        olds = [old0[:], old1[:], old2[:], old3[:]]
         news = []
         for t in range(PACK):
-            acc = product(q4, (z_codes, z_scales), t)
+            acc = product(q4, (z_codes, z_scales), t, "acc", 6)
             new = keep.tile([P, S], F32, name=f"new{t}")
             nc.vector.scalar_tensor_tensor(new[:], olds[t], 0.5, acc[:], ALU.mult, ALU.max)
             news.append(new)

@@ -25,6 +25,7 @@ def tile_picked_triopullbputbpagex_none_p_kernel(tc, x_words, x_scales, w1, w2, 
     with ExitStack() as ctx:
         lists = ctx.enter_context(tc.tile_pool(name="lists", bufs=1))
         keep = ctx.enter_context(tc.tile_pool(name="keep", bufs=1))
+        shared = ctx.enter_context(tc.tile_pool(name="shared", bufs=1))
         psum = ctx.enter_context(tc.psum_pool(name="psum", bufs=1))
 
         def load_list(name, src):
@@ -44,14 +45,15 @@ def tile_picked_triopullbputbpagex_none_p_kernel(tc, x_words, x_scales, w1, w2, 
         l_two = load_list("l_two", two)
         nc.sync.dma_start(out=xw[:], in_=x_words[0].rearrange("p n t -> p (n t)").bitcast(I32))
         for q in range(4):
-            nc.scalar.dma_start(out=xs[32 * q : 32 * q + 4, :].bitcast(I32), in_=x_scales[0, 4 * q : 4 * q + 4, :].bitcast(I32))
+            nc.sync.dma_start(out=xs[32 * q : 32 * q + 4, :].bitcast(I32), in_=x_scales[0, 4 * q : 4 * q + 4, :].bitcast(I32))
         warm = keep.tile([P, 2], F32, name="warm")
         nc.gpsimd.memset(warm[:, 0:1], 0.0)
         nc.scalar.activation(warm[:, 1:2], warm[:, 0:1], ACT.Sigmoid)
         l_offs = load_list("l_offs", offs)
         w2_raw = load_weight("w2", w2, nc.sync)
         l_three = load_list("l_three", three)
-        w1_raw = load_weight("w1", w1, nc.sync)
+        w1_raw = shared.tile([P, PACK, H], F32, name="w1_raw", offset=0)
+        nc.sync.dma_start(out=w1_raw[:], in_=w1.rearrange("(p j) c -> p j c", j=PACK))
         l_n2 = load_list("l_n2", n2)
         l_n1 = load_list("l_n1", n1)
         gain = keep.tile([P, PACK], F32, name="gain")
@@ -69,8 +71,8 @@ def tile_picked_triopullbputbpagex_none_p_kernel(tc, x_words, x_scales, w1, w2, 
             nc.sync.dma_start(out=page[:], in_=mem_rows[t])
             pages.append(page)
 
-        def pick_scales(name, offsets):
-            picked = keep.tile([P, S], U8, name=name + "_scales", align_bytes=64)
+        def pick_scales(name, offsets, tag):
+            picked = keep.tile([P, S], U8, name=name + "_scales", tag=tag, align_bytes=64)
             nc.vector.tensor_copy(picked[:], xs[:].indirect(offsets[:]))
             return picked
 
@@ -87,8 +89,8 @@ def tile_picked_triopullbputbpagex_none_p_kernel(tc, x_words, x_scales, w1, w2, 
             )
             return grouped
 
-        def quantize(name, grouped):
-            codes = keep.tile([P, H], U32, name=name + "_codes", align_bytes=64)
+        def quantize(name, grouped, tag=None):
+            codes = keep.tile([P, H], U32, name=name + "_codes", tag=tag or name + "_codes", align_bytes=64)
             scales = keep.tile([P, H], U8, name=name + "_qs", align_bytes=64)
             nc.vector.quantize_mx(out=codes[:].bitcast(FP8X4), scales=scales[:], in_=grouped[:])
             return codes, scales
@@ -107,13 +109,13 @@ def tile_picked_triopullbputbpagex_none_p_kernel(tc, x_words, x_scales, w1, w2, 
             )
             return acc
 
-        s_two = pick_scales("two", l_two)
-        s_offs = pick_scales("offs", l_offs)
-        s_three = pick_scales("three", l_three)
-        x_two = (pick_words("two", l_two, "two_words"), s_two)
+        w_two = pick_words("two", l_two, "two_words")
+        w_offs = pick_words("offs", l_offs, "offs_words")
+        w_three = pick_words("three", l_three, "three_words")
+        x_two = (w_two, pick_scales("two", l_two, "two_scales"))
         q2 = quantize("w2", round_weight("w2", w2_raw, "w2_grouped"))
-        x_offs = (pick_words("offs", l_offs, "offs_words"), s_offs)
-        x_three = (pick_words("three", l_three, "w2_grouped"), s_three)
+        x_offs = (w_offs, pick_scales("offs", l_offs, "offs_scales"))
+        x_three = (w_three, pick_scales("three", l_three, "w2_grouped"))
 
         def fetch(name, window, offsets, tag):
             picked = keep.tile([P, S], F32, name=name, tag=tag, align_bytes=64)
@@ -124,8 +126,8 @@ def tile_picked_triopullbputbpagex_none_p_kernel(tc, x_words, x_scales, w1, w2, 
         q1 = quantize("w1", round_weight("w1", w1_raw, "w1_grouped"))
         gates = []
         for t in range(PACK):
-            acc = product(q2, x_two, t, "d_acc", 2)
-            d_win = keep.tile([P, S], F32, name=f"d_win{t}", tag=("w1_raw", "w1_grouped", "d_win2", "d_win3")[t], align_bytes=64)
+            acc = product(q2, x_two, t, "acc", 8)
+            d_win = shared.tile([P, S], F32, name=f"d_win{t}", offset=4 * S * t)
             nc.scalar.copy(out=d_win[:], in_=acc[:])
             dd = fetch(f"dd{t}", d_win, l_n2, f"dd{t}")
             nc.gpsimd.tensor_tensor(dd[:], dd[:], d_win[:], ALU.subtract)
@@ -133,58 +135,79 @@ def tile_picked_triopullbputbpagex_none_p_kernel(tc, x_words, x_scales, w1, w2, 
 
         zg = keep.tile([P, S, PACK], BF16, name="zg", tag="zg", align_bytes=64)
         dys = []
-        y_wins = []
+        q3 = quantize("w3", round_weight("w3", w3_raw, "two_words"))
         for t in range(PACK):
-            acc = product(q1, x_offs, t, "acc", 6)
+            acc = product(q1, x_offs, t, "acc", 8)
             y_win = keep.tile([P, S], F32, name=f"y_win{t}")
             nc.scalar.activation(y_win[:], acc[:], ACT.Copy, scale=gain[:, t : t + 1])
-            y_wins.append(y_win)
-        for t in range(PACK - 1):
-            dys.append((y_wins[t], fetch(f"dy{t}", y_wins[t], l_n1, f"dy{t}")))
-        q3 = quantize("w3", round_weight("w3", w3_raw, "w1_grouped"))
-        dys.append((y_wins[3], fetch("dy3", y_wins[3], l_n1, "w1_grouped")))
+            dys.append((y_win, fetch(f"dy{t}", y_win, l_n1, f"dy{t}")))
+        y_win, dy = dys[3]
+        nc.vector.scalar_tensor_tensor(dy[:], acc[:], gain[:, 3:4], dy[:], ALU.mult, ALU.subtract)
         for t in range(PACK):
             nc.scalar.activation(gates[t][:], gates[t][:], ACT.Sigmoid)
         bs = []
         for t in range(PACK):
-            acc = product(q3, x_three, t, "acc", 6)
+            acc = product(q3, x_three, t, "acc", 8)
             b_win = keep.tile([P, S], F32, name=f"b_win{t}", tag=f"b_win{t}", align_bytes=64)
             nc.scalar.activation(b_win[:], acc[:], ACT.Copy, scale=gain[:, t : t + 1])
-            b_picked = keep.tile([P, W], F32, name=f"b_picked{t}", tag=f"b_picked{t}")
+            b_picked = keep.tile([P, W], F32, name=f"b_picked{t}", tag=f"b_picked{t}", align_bytes=64)
             nc.vector.tensor_copy(b_picked[:], b_win[:].indirect(l_n4[:]))
             bs.append(b_picked)
-        for t in range(PACK):
-            y_win, dy = dys[t]
-            last = t >= PACK - 2
-            nc.gpsimd.tensor_tensor(dy[:], dy[:], y_win[:], ALU.subtract)
-            nc.gpsimd.tensor_tensor(dy[:], dy[:], gates[t][:], ALU.mult)
-            m1 = keep.tile([P, S], F32, name=f"m1_{t}")
-            (nc.vector if last else nc.gpsimd).tensor_tensor(m1[:], dy[:], y_win[:], ALU.add)
-            m_picked = keep.tile([P, W], F32, name=f"m_picked{t}", tag=f"m_picked{t}")
-            nc.vector.tensor_scalar(m_picked[:], m1[:].indirect(l_n3[:]), -0.5, 0.0, ALU.mult, ALU.add)
-            if last:
-                nc.vector.tensor_tensor(m1[:].indirect(l_n3[:]), m_picked[:], bs[t][:], ALU.add)
-            else:
-                nc.gpsimd.tensor_tensor(m_picked[:], m_picked[:], bs[t][:], ALU.add)
-                nc.vector.tensor_copy(m1[:].indirect(l_n3[:]), m_picked[:])
-            nc.scalar.copy(out=zg[:, :, t], in_=m1[:])
+        def tile32(name, tag, width=S, bufs=1):
+            return keep.tile([P, width], F32, name=name, tag=tag, bufs=bufs, align_bytes=64)
 
-        q4 = quantize("w4", round_weight("w4", w4_raw, "d_win3"))
-        old0 = keep.tile([P, S], F32, name="old0", tag="dy1", align_bytes=64)
-        old1 = keep.tile([P, S], F32, name="old1", tag="b_picked3")
-        old2 = keep.tile([P, S], F32, name="old2", tag="m_picked3")
-        nc.vector.tensor_copy(old0[:], pages[0][:].indirect(l_n5[:]))
+        def own_minus_picked(t):
+            diff = tile32(f"diff{t}", "diff", bufs=2)
+            nc.gpsimd.tensor_tensor(diff[:], dys[t][0][:], dys[t][1][:], ALU.subtract)
+            return diff
+
+        def pick_half(t, m1):
+            m_picked = tile32(f"m_picked{t}", f"m_picked{t}", W)
+            nc.vector.tensor_scalar(m_picked[:], m1[:].indirect(l_n3[:]), -0.5, 0.0, ALU.mult, ALU.add)
+            return m_picked
+
+        first, second = (0, 1), (2, 3)
+        diffs = [own_minus_picked(t) for t in first]
+        for t in first:
+            nc.gpsimd.tensor_tensor(diffs[t][:], diffs[t][:], gates[t][:], ALU.mult)
+        m1s = []
+        for t in first:
+            m1s.append(tile32(f"m1_{t}", f"m1_{t}"))
+            nc.gpsimd.tensor_tensor(m1s[t][:], dys[t][0][:], diffs[t][:], ALU.subtract)
+        diffs = diffs + [own_minus_picked(2), dys[3][1]]
+        halves = [pick_half(t, m1s[t]) for t in first]
+        old1 = tile32("old1", "diff", bufs=2)
         nc.vector.tensor_copy(old1[:], pages[1][:].indirect(l_n5[:]))
+        for t in first:
+            nc.gpsimd.tensor_tensor(halves[t][:], halves[t][:], bs[t][:], ALU.add)
+        for t in first:
+            nc.vector.tensor_copy(m1s[t][:].indirect(l_n3[:]), halves[t][:])
+            nc.scalar.copy(out=zg[:, :, t], in_=m1s[t][:])
+        pulls = [None, None, tile32("pull2", "b_picked1"), tile32("pull3", "dd2")]
+        for t in second:
+            nc.gpsimd.tensor_tensor(pulls[t][:], diffs[t][:], gates[t][:], ALU.mult)
+        m1s = m1s + [tile32("m1_2", "dd3"), tile32("m1_3", "m1_3")]
+        for t in second:
+            nc.vector.tensor_tensor(m1s[t][:], dys[t][0][:], pulls[t][:], ALU.subtract)
+        halves = halves + [pick_half(t, m1s[t]) for t in second]
+        for t in second:
+            nc.vector.tensor_tensor(m1s[t][:].indirect(l_n3[:]), halves[t][:], bs[t][:], ALU.add)
+            nc.scalar.copy(out=zg[:, :, t], in_=m1s[t][:])
+
+        q4 = quantize("w4", round_weight("w4", w4_raw, "b_win0"), "b_picked2")
+        old0 = keep.tile([P, S], F32, name="old0", tag="b_win2", align_bytes=64)
+        old2 = keep.tile([P, S], F32, name="old2", tag="m_picked2", align_bytes=64)
+        nc.vector.tensor_copy(old0[:], pages[0][:].indirect(l_n5[:]))
         nc.vector.tensor_copy(old2[:], pages[2][:].indirect(l_n5[:]))
         z_codes = keep.tile([P, S], U32, name="z_codes", align_bytes=64)
         z_scales = keep.tile([P, S], U8, name="z_scales", align_bytes=64)
         nc.vector.quantize_mx(out=z_codes[:].bitcast(FP8X4), scales=z_scales[:], in_=zg[:].rearrange("p s t -> p (s t)"))
-        old3 = keep.tile([P, S], F32, name="old3", tag="zg", align_bytes=64)
+        old3 = keep.tile([P, S], F32, name="old3", tag="m1_3", align_bytes=64)
         nc.vector.tensor_copy(old3[:], pages[3][:].indirect(l_n5[:]))
         olds = [old0[:], old1[:], old2[:], old3[:]]
         news = []
         for t in range(PACK):
-            acc = product(q4, (z_codes, z_scales), t, "acc", 6)
+            acc = product(q4, (z_codes, z_scales), t, "acc", 8)
             new = keep.tile([P, S], F32, name=f"new{t}")
             nc.vector.scalar_tensor_tensor(new[:], olds[t], 0.5, acc[:], ALU.mult, ALU.max)
             news.append(new)

@@ -26,6 +26,7 @@ def tile_picked_triopullbputbpagex_none_p_kernel(tc, x_words, x_scales, w1, w2, 
         lists = ctx.enter_context(tc.tile_pool(name="lists", bufs=1))
         keep = ctx.enter_context(tc.tile_pool(name="keep", bufs=1))
         shared = ctx.enter_context(tc.tile_pool(name="shared", bufs=1))
+        late = ctx.enter_context(tc.tile_pool(name="late", bufs=1))
         psum = ctx.enter_context(tc.psum_pool(name="psum", bufs=1))
 
         def load_list(name, src):
@@ -148,7 +149,10 @@ def tile_picked_triopullbputbpagex_none_p_kernel(tc, x_words, x_scales, w1, w2, 
         bs = []
         for t in range(PACK):
             acc = product(q3, x_three, t, "acc", 8)
-            b_win = keep.tile([P, S], F32, name=f"b_win{t}", tag=f"b_win{t}", align_bytes=64)
+            if t < 3:
+                b_win = keep.tile([P, S], F32, name=f"b_win{t}", tag=f"b_win{t}", align_bytes=64)
+            else:
+                b_win = late.tile([P, S], F32, name="b_win3", offset=8 * S - 64)
             nc.scalar.activation(b_win[:], acc[:], ACT.Copy, scale=gain[:, t : t + 1])
             b_picked = keep.tile([P, W], F32, name=f"b_picked{t}", tag=f"b_picked{t}", align_bytes=64)
             nc.vector.tensor_copy(b_picked[:], b_win[:].indirect(l_n4[:]))
@@ -162,8 +166,8 @@ def tile_picked_triopullbputbpagex_none_p_kernel(tc, x_words, x_scales, w1, w2, 
             return diff
 
         def pick_half(t, m1):
-            m_picked = tile32(f"m_picked{t}", f"m_picked{t}", W)
-            nc.vector.tensor_scalar(m_picked[:], m1[:].indirect(l_n3[:]), -0.5, 0.0, ALU.mult, ALU.add)
+            m_picked = early_halves[:, t, :] if t < 2 else tile32(f"m_picked{t}", f"m_picked{t}", W)[:]
+            nc.vector.tensor_scalar(m_picked, m1[:].indirect(l_n3[:]), -0.5, 0.0, ALU.mult, ALU.add)
             return m_picked
 
         first, second = (0, 1), (2, 3)
@@ -175,13 +179,16 @@ def tile_picked_triopullbputbpagex_none_p_kernel(tc, x_words, x_scales, w1, w2, 
             m1s.append(tile32(f"m1_{t}", f"m1_{t}"))
             nc.gpsimd.tensor_tensor(m1s[t][:], dys[t][0][:], diffs[t][:], ALU.subtract)
         diffs = diffs + [own_minus_picked(2), dys[3][1]]
+        early_olds = late.tile([P, 2, S], F32, name="early_olds", offset=0)
+        early_halves = late.tile([P, 2, W], F32, name="early_halves", offset=8 * S)
+        old0, old1 = early_olds[:, 0, :], early_olds[:, 1, :]
+        nc.vector.tensor_copy(old0, pages[0][:].indirect(l_n5[:]))
         halves = [pick_half(t, m1s[t]) for t in first]
-        old1 = tile32("old1", "diff", bufs=2)
-        nc.vector.tensor_copy(old1[:], pages[1][:].indirect(l_n5[:]))
+        nc.vector.tensor_copy(old1, pages[1][:].indirect(l_n5[:]))
         for t in first:
-            nc.gpsimd.tensor_tensor(halves[t][:], halves[t][:], bs[t][:], ALU.add)
+            nc.gpsimd.tensor_tensor(halves[t], halves[t], bs[t][:], ALU.add)
         for t in first:
-            nc.vector.tensor_copy(m1s[t][:].indirect(l_n3[:]), halves[t][:])
+            nc.vector.tensor_copy(m1s[t][:].indirect(l_n3[:]), halves[t])
             nc.scalar.copy(out=zg[:, :, t], in_=m1s[t][:])
         pulls = [None, None, tile32("pull2", "b_picked1"), tile32("pull3", "dd2")]
         for t in second:
@@ -191,26 +198,33 @@ def tile_picked_triopullbputbpagex_none_p_kernel(tc, x_words, x_scales, w1, w2, 
             nc.vector.tensor_tensor(m1s[t][:], dys[t][0][:], pulls[t][:], ALU.subtract)
         halves = halves + [pick_half(t, m1s[t]) for t in second]
         for t in second:
-            nc.vector.tensor_tensor(m1s[t][:].indirect(l_n3[:]), halves[t][:], bs[t][:], ALU.add)
+            nc.vector.tensor_tensor(m1s[t][:].indirect(l_n3[:]), halves[t], bs[t][:], ALU.add)
             nc.scalar.copy(out=zg[:, :, t], in_=m1s[t][:])
 
-        q4 = quantize("w4", round_weight("w4", w4_raw, "b_win0"), "b_picked2")
-        old0 = keep.tile([P, S], F32, name="old0", tag="b_win2", align_bytes=64)
-        old2 = keep.tile([P, S], F32, name="old2", tag="m_picked2", align_bytes=64)
-        nc.vector.tensor_copy(old0[:], pages[0][:].indirect(l_n5[:]))
-        nc.vector.tensor_copy(old2[:], pages[2][:].indirect(l_n5[:]))
+        q4 = quantize("w4", round_weight("w4", w4_raw, "b_win1"), "b_picked2")
+        old2 = tile32("old2", "m_picked2")
+        nc.vector.tensor_scalar(old2[:], pages[2][:].indirect(l_n5[:]), 0.5, 0.0, ALU.mult, ALU.add)
         z_codes = keep.tile([P, S], U32, name="z_codes", align_bytes=64)
         z_scales = keep.tile([P, S], U8, name="z_scales", align_bytes=64)
         nc.vector.quantize_mx(out=z_codes[:].bitcast(FP8X4), scales=z_scales[:], in_=zg[:].rearrange("p s t -> p (s t)"))
-        old3 = keep.tile([P, S], F32, name="old3", tag="m1_3", align_bytes=64)
-        nc.vector.tensor_copy(old3[:], pages[3][:].indirect(l_n5[:]))
-        olds = [old0[:], old1[:], old2[:], old3[:]]
+        old3 = tile32("old3", "m1_3")
+        nc.vector.tensor_scalar(old3[:], pages[3][:].indirect(l_n5[:]), 0.5, 0.0, ALU.mult, ALU.add)
+        olds = [old0, old1, old2[:], old3[:]]
         news = []
         for t in range(PACK):
             acc = product(q4, (z_codes, z_scales), t, "acc", 8)
             new = keep.tile([P, S], F32, name=f"new{t}")
-            nc.vector.scalar_tensor_tensor(new[:], olds[t], 0.5, acc[:], ALU.mult, ALU.max)
+            if t in first:
+                nc.vector.scalar_tensor_tensor(new[:], olds[t], 0.5, acc[:], ALU.mult, ALU.max)
+            else:
+                nc.scalar.copy(out=new[:], in_=acc[:])
             news.append(new)
-        for t in range(PACK):
+        for t in second:
+            nc.gpsimd.tensor_tensor(olds[t], olds[t], news[t][:], ALU.subtract)
+            nc.scalar.activation(olds[t], olds[t], ACT.Relu)
+        for t in first:
             nc.vector.tensor_copy(pages[t][:].indirect(l_n5[:]), news[t][:])
+            nc.sync.dma_start(out=out_rows[t], in_=pages[t][:])
+        for t in second:
+            nc.vector.tensor_tensor(pages[t][:].indirect(l_n5[:]), news[t][:], olds[t], ALU.add)
             nc.sync.dma_start(out=out_rows[t], in_=pages[t][:])

from contextlib import ExitStack

import concourse.mybir as mybir

K, T, S, N, H, W, U = 512, 2048, 512, 512, 512, 256, 1024
FLOPS = 2 * 3 * K * H * S + 2 * H * N * S

F32 = mybir.dt.float32
BF16 = mybir.dt.bfloat16
I32 = mybir.dt.int32
U32 = mybir.dt.uint32
U16 = mybir.dt.uint16
U8 = mybir.dt.uint8
FP8X4 = mybir.dt.float8_e4m3fn_x4
ALU = mybir.AluOpType
ACT = mybir.ActivationFunctionType

P = 128
PACK = 4
HALF = S // 2


def tile_picked_triopullbputbpagex_none_p_kernel(tc, x_words, x_scales, w1, w2, w3, gn, w4, mem, offs, two, three, n1, n2, n3, n4, n5, out):
    nc = tc.nc
    with ExitStack() as ctx:
        lists = ctx.enter_context(tc.tile_pool(name="lists", bufs=1))
        keep = ctx.enter_context(tc.tile_pool(name="keep", bufs=1))
        shared = ctx.enter_context(tc.tile_pool(name="shared", bufs=1))
        late = ctx.enter_context(tc.tile_pool(name="late", bufs=1))
        psum = ctx.enter_context(tc.psum_pool(name="psum", bufs=1))

        def load_list(name, src):
            tile = lists.tile(list(src.shape), U16, name=name)
            nc.sync.dma_start(tile[:], src)
            return tile

        def load_weight(name, src, queue):
            raw = keep.tile([P, PACK, H], F32, name=name + "_raw", tag=name + "_raw", align_bytes=64)
            queue.dma_start(out=raw[:], in_=src.rearrange("(p j) c -> p j c", j=PACK))
            return raw

        xs = keep.tile([P, T], U8, name="xs")
        xw = keep.tile([P, T], I32, name="xw")
        nc.gpsimd.memset(xs[:].bitcast(I32), 0)

        l_two = load_list("l_two", two)
        nc.sync.dma_start(out=xw[:], in_=x_words[0].rearrange("p n t -> p (n t)").bitcast(I32))
        for q in range(4):
            nc.sync.dma_start(out=xs[32 * q : 32 * q + 4, :].bitcast(I32), in_=x_scales[0, 4 * q : 4 * q + 4, :].bitcast(I32))
        warm = keep.tile([P, 2], F32, name="warm")
        nc.gpsimd.memset(warm[:, 0:1], 0.0)
        nc.scalar.activation(warm[:, 1:2], warm[:, 0:1], ACT.Sigmoid)
        l_offs = load_list("l_offs", offs)
        w2_raw = load_weight("w2", w2, nc.sync)
        l_three = load_list("l_three", three)
        w1_raw = shared.tile([P, PACK, H], F32, name="w1_raw", offset=0)
        nc.sync.dma_start(out=w1_raw[:], in_=w1.rearrange("(p j) c -> p j c", j=PACK))
        l_n2 = load_list("l_n2", n2)
        l_n1 = load_list("l_n1", n1)
        gain = keep.tile([P, PACK], F32, name="gain")
        nc.sync.dma_start(out=gain[:], in_=gn.rearrange("(p t) o -> p (t o)", t=PACK))
        w3_raw = load_weight("w3", w3, nc.sync)
        l_n4 = load_list("l_n4", n4)
        l_n3 = load_list("l_n3", n3)
        l_n5 = load_list("l_n5", n5)
        w4_raw = load_weight("w4", w4, nc.sync)
        mem_rows = mem.rearrange("(p t) u -> t p u", t=PACK)
        out_rows = out.rearrange("(p t) u -> t p u", t=PACK)
        pages = []
        for t in range(PACK):
            page = keep.tile([P, U], F32, name=f"page{t}")
            nc.sync.dma_start(out=page[:], in_=mem_rows[t])
            pages.append(page)

        def pick_scales(name, offsets, tag):
            picked = keep.tile([P, S], U8, name=name + "_scales", tag=tag, align_bytes=64)
            nc.vector.tensor_copy(picked[:], xs[:].indirect(offsets[:]))
            return picked

        def pick_words(name, offsets, tag):
            picked = keep.tile([P, S], U32, name=name + "_words", tag=tag, align_bytes=64)
            nc.vector.tensor_copy(picked[:], xw[:].bitcast(U32).indirect(offsets[:]))
            return picked

        def round_weight(name, raw, tag):
            grouped = keep.tile([P, PACK * H], BF16, name=name + "_grouped", tag=tag, align_bytes=64)
            nc.scalar.copy(
                out=grouped[:].rearrange("p (t m j) -> p m j t", t=PACK, j=PACK),
                in_=raw[:].rearrange("p j (m t) -> p m j t", t=PACK),
            )
            return grouped

        def quantize(name, grouped, tag=None):
            codes = keep.tile([P, H], U32, name=name + "_codes", tag=tag or name + "_codes", align_bytes=64)
            scales = keep.tile([P, H], U8, name=name + "_qs", align_bytes=64)
            nc.vector.quantize_mx(out=codes[:].bitcast(FP8X4), scales=scales[:], in_=grouped[:])
            return codes, scales

        def product(weight, moving, t, tag, depth):
            acc = psum.tile([P, S], F32, name=tag, bufs=depth)
            cols = slice(P * t, P * (t + 1))
            nc.tensor.matmul_mx(
                out=acc[:],
                lhsT=weight[0][:, cols].bitcast(FP8X4),
                lhsT_scale=weight[1][:, cols],
                rhs=moving[0][:].bitcast(FP8X4),
                rhs_scale=moving[1][:],
                start=True,
                stop=True,
            )
            return acc

        w_two = pick_words("two", l_two, "two_words")
        w_offs = pick_words("offs", l_offs, "offs_words")
        w_three = pick_words("three", l_three, "three_words")
        x_two = (w_two, pick_scales("two", l_two, "two_scales"))
        q2 = quantize("w2", round_weight("w2", w2_raw, "w2_grouped"))
        x_offs = (w_offs, pick_scales("offs", l_offs, "offs_scales"))
        x_three = (w_three, pick_scales("three", l_three, "w2_grouped"))

        def fetch(name, window, offsets, tag):
            picked = keep.tile([P, S], F32, name=name, tag=tag, align_bytes=64)
            for a in range(2):
                nc.vector.tensor_copy(picked[:, HALF * a : HALF * (a + 1)], window[:].indirect(offsets[:, 16 * a : 16 * (a + 1)]))
            return picked

        q1 = quantize("w1", round_weight("w1", w1_raw, "w1_grouped"))
        gates = []
        for t in range(PACK):
            acc = product(q2, x_two, t, "acc", 8)
            d_win = shared.tile([P, S], F32, name=f"d_win{t}", offset=4 * S * t)
            nc.scalar.copy(out=d_win[:], in_=acc[:])
            dd = fetch(f"dd{t}", d_win, l_n2, f"dd{t}")
            nc.gpsimd.tensor_tensor(dd[:], dd[:], d_win[:], ALU.subtract)
            gates.append(dd)

        zg = keep.tile([P, S, PACK], BF16, name="zg", tag="zg", align_bytes=64)
        dys = []
        q3 = quantize("w3", round_weight("w3", w3_raw, "two_words"))
        for t in range(PACK):
            acc = product(q1, x_offs, t, "acc", 8)
            y_win = keep.tile([P, S], F32, name=f"y_win{t}")
            nc.scalar.activation(y_win[:], acc[:], ACT.Copy, scale=gain[:, t : t + 1])
            dys.append((y_win, fetch(f"dy{t}", y_win, l_n1, f"dy{t}")))
        y_win, dy = dys[3]
        nc.vector.scalar_tensor_tensor(dy[:], acc[:], gain[:, 3:4], dy[:], ALU.mult, ALU.subtract)
        for t in range(PACK):
            nc.scalar.activation(gates[t][:], gates[t][:], ACT.Sigmoid)
        bs = []
        for t in range(PACK):
            acc = product(q3, x_three, t, "acc", 8)
            if t < 3:
                b_win = keep.tile([P, S], F32, name=f"b_win{t}", tag=f"b_win{t}", align_bytes=64)
            else:
                b_win = late.tile([P, S], F32, name="b_win3", offset=8 * S - 64)
            nc.scalar.activation(b_win[:], acc[:], ACT.Copy, scale=gain[:, t : t + 1])
            b_picked = keep.tile([P, W], F32, name=f"b_picked{t}", tag=f"b_picked{t}", align_bytes=64)
            nc.vector.tensor_copy(b_picked[:], b_win[:].indirect(l_n4[:]))
            bs.append(b_picked)
        def tile32(name, tag, width=S, bufs=1):
            return keep.tile([P, width], F32, name=name, tag=tag, bufs=bufs, align_bytes=64)

        def own_minus_picked(t):
            diff = tile32(f"diff{t}", "diff", bufs=2)
            nc.gpsimd.tensor_tensor(diff[:], dys[t][0][:], dys[t][1][:], ALU.subtract)
            return diff

        def pick_half(t, m1):
            m_picked = early_halves[:, t, :] if t < 2 else tile32(f"m_picked{t}", f"m_picked{t}", W)[:]
            nc.vector.tensor_scalar(m_picked, m1[:].indirect(l_n3[:]), -0.5, 0.0, ALU.mult, ALU.add)
            return m_picked

        first, second = (0, 1), (2, 3)
        diffs = [own_minus_picked(t) for t in first]
        for t in first:
            nc.gpsimd.tensor_tensor(diffs[t][:], diffs[t][:], gates[t][:], ALU.mult)
        m1s = []
        for t in first:
            m1s.append(tile32(f"m1_{t}", f"m1_{t}"))
            nc.gpsimd.tensor_tensor(m1s[t][:], dys[t][0][:], diffs[t][:], ALU.subtract)
        diffs = diffs + [own_minus_picked(2), dys[3][1]]
        early_olds = late.tile([P, 2, S], F32, name="early_olds", offset=0)
        early_halves = late.tile([P, 2, W], F32, name="early_halves", offset=8 * S)
        old0, old1 = early_olds[:, 0, :], early_olds[:, 1, :]
        nc.vector.tensor_copy(old0, pages[0][:].indirect(l_n5[:]))
        halves = [pick_half(t, m1s[t]) for t in first]
        nc.vector.tensor_copy(old1, pages[1][:].indirect(l_n5[:]))
        for t in first:
            nc.gpsimd.tensor_tensor(halves[t], halves[t], bs[t][:], ALU.add)
        for t in first:
            nc.vector.tensor_copy(m1s[t][:].indirect(l_n3[:]), halves[t])
            nc.scalar.copy(out=zg[:, :, t], in_=m1s[t][:])
        pulls = [None, None, tile32("pull2", "b_picked1"), tile32("pull3", "dd2")]
        for t in second:
            nc.gpsimd.tensor_tensor(pulls[t][:], diffs[t][:], gates[t][:], ALU.mult)
        m1s = m1s + [tile32("m1_2", "dd3"), tile32("m1_3", "m1_3")]
        for t in second:
            nc.vector.tensor_tensor(m1s[t][:], dys[t][0][:], pulls[t][:], ALU.subtract)
        halves = halves + [pick_half(t, m1s[t]) for t in second]
        for t in second:
            nc.vector.tensor_tensor(m1s[t][:].indirect(l_n3[:]), halves[t], bs[t][:], ALU.add)
            nc.scalar.copy(out=zg[:, :, t], in_=m1s[t][:])

        q4 = quantize("w4", round_weight("w4", w4_raw, "b_win1"), "b_picked2")
        old2 = tile32("old2", "m_picked2")
        nc.vector.tensor_scalar(old2[:], pages[2][:].indirect(l_n5[:]), 0.5, 0.0, ALU.mult, ALU.add)
        z_codes = keep.tile([P, S], U32, name="z_codes", align_bytes=64)
        z_scales = keep.tile([P, S], U8, name="z_scales", align_bytes=64)
        nc.vector.quantize_mx(out=z_codes[:].bitcast(FP8X4), scales=z_scales[:], in_=zg[:].rearrange("p s t -> p (s t)"))
        old3 = tile32("old3", "m1_3")
        nc.vector.tensor_scalar(old3[:], pages[3][:].indirect(l_n5[:]), 0.5, 0.0, ALU.mult, ALU.add)
        olds = [old0, old1, old2[:], old3[:]]
        news = []
        for t in range(PACK):
            acc = product(q4, (z_codes, z_scales), t, "acc", 8)
            new = keep.tile([P, S], F32, name=f"new{t}")
            if t in first:
                nc.vector.scalar_tensor_tensor(new[:], olds[t], 0.5, acc[:], ALU.mult, ALU.max)
            else:
                nc.scalar.copy(out=new[:], in_=acc[:])
            news.append(new)
        for t in second:
            nc.gpsimd.tensor_tensor(olds[t], olds[t], news[t][:], ALU.subtract)
            nc.scalar.activation(olds[t], olds[t], ACT.Relu)
        for t in first:
            nc.vector.tensor_copy(pages[t][:].indirect(l_n5[:]), news[t][:])
            nc.sync.dma_start(out=out_rows[t], in_=pages[t][:])
        for t in second:
            nc.vector.tensor_tensor(pages[t][:].indirect(l_n5[:]), news[t][:], olds[t], ALU.add)
            nc.sync.dma_start(out=out_rows[t], in_=pages[t][:])
